import numpy as np
import ml_dtypes


def mxq(x, axis, fmt="e4m3"):
    dtype, down = {"e4m3": (ml_dtypes.float8_e4m3fn, 7), "e5m2": (ml_dtypes.float8_e5m2, 14)}[fmt]
    v = np.moveaxis(np.asarray(x, np.float32).astype(ml_dtypes.bfloat16).astype(np.float64), axis, -1)
    blocks = v.reshape(v.shape[:-1] + (-1, 32))
    amax = np.abs(blocks).max(-1, keepdims=True)
    byte = np.maximum(np.where(amax > 0, np.frexp(amax)[1] - 1 + 127, 0) - down, 1)
    scale = np.exp2(byte - 127.0)
    codes = (blocks / scale).astype(np.float32).astype(dtype).astype(np.float64)
    return np.moveaxis((codes * scale).reshape(v.shape), -1, axis)


WIDE = False


def mx_kscale(k):
    if not WIDE:
        return np.ones(k)
    levels = np.array([10, -10, 5, -5, 0])
    if k % 512:
        return np.exp2(np.random.permutation(np.resize(levels, k // 32))).repeat(32)
    a = np.empty((k // 512, 16))
    for p in range(k // 512):
        a[p, :8] = np.random.permutation(np.resize(levels, 8))
        for g in range(8):
            far = levels[np.abs(levels - a[p, g]) >= 10]
            a[p, g + 8] = far[np.random.randint(len(far))]
    return np.exp2(a.ravel()).repeat(32)


def f64(x):
    return np.asarray(x).astype(np.float64)


def striped(idx):
    return np.tile(idx.reshape(-1, 16).T, (8, 1)).astype(np.uint16)


def unstriped(offs):
    return offs[:16].T.reshape(-1).astype(np.int64)


def striped8(idx):
    return np.concatenate([x.reshape(-1, 16).T for x in idx]).astype(np.uint16)


def runs(offs, k):
    lists = np.stack([offs[16 * r : 16 * r + 16].T.reshape(-1) for r in range(8)]).astype(np.int64)
    return lists[np.arange(k) % 512 // 64]


def pack_weight(w):
    k, n = w.shape
    w = f64(np.asarray(w, np.float32).astype(ml_dtypes.bfloat16)).reshape(k // 32, 32, n)
    amax = np.abs(w).max(1)
    byte = np.clip(np.where(amax > 0, np.frexp(amax)[1] - 1 + 127 - 7, 1), 1, 254)
    scaled = (w * np.exp2(127.0 - byte)[:, None, :]).reshape(k, n).astype(np.float32)
    words = np.ascontiguousarray(scaled.reshape(k // 512, 128, 4, n).transpose(0, 1, 3, 2)).astype(ml_dtypes.float8_e4m3fn).view(np.uint8)
    return words, np.ascontiguousarray(byte.astype(np.uint8).reshape(k // 512, 16, n))


def unpack_weight(words, scales):
    g, p, n, _ = words.shape
    vals = np.ascontiguousarray(words).view(ml_dtypes.float8_e4m3fn).astype(np.float64) * np.repeat(np.exp2(scales.astype(np.float64) - 127.0), 8, axis=1)[..., None]
    return vals.transpose(0, 1, 3, 2).reshape(g * 512, n)


K, T, S, N, H = 512, 2048, 512, 512, 512


def setup_inputs():
    n = np.random.standard_normal
    s = mx_kscale(K)[:, None]
    u = mx_kscale(H)
    packed_xT = pack_weight(n((K, T)) * s)
    return {
        "x_words": packed_xT[0],
        "x_scales": packed_xT[1],
        "w1": (n((K, H)) / np.sqrt(K) / s).astype(np.float32),
        "gn": (np.random.uniform(0.5, 1.5, (H, 1)) * u[:, None]).astype(np.float32),
        "w2": (n((H, N)) / np.sqrt(H) / u[:, None]).astype(np.float32),
        "offs": striped(np.random.permutation(T)[:S]),
        "n1": striped8(np.stack([np.random.permutation(S) for _ in range(8)])),
        "n2": striped8(np.stack([np.random.permutation(S) for _ in range(8)])),
        "n3": striped8(np.stack([np.random.permutation(S) for _ in range(8)])),
        "n4": striped8(np.stack([np.random.permutation(S) for _ in range(8)])),
    }


def reference(x_words, x_scales, w1, gn, w2, offs, n1, n2, n3, n4):
    xq = unpack_weight(x_words, x_scales)[:, unstriped(offs)]
    y = mxq(f64(w1), 0, "e4m3").T @ xq
    z = f64(gn) * (np.minimum(np.maximum(y, y[np.arange(H)[:, None], runs(n1, H)]), y[np.arange(H)[:, None], runs(n2, H)]))
    h = mxq(f64(w2), 0, "e4m3").T @ mxq(z, 0, "e4m3")
    return h * (np.tanh(y[np.arange(H)[:, None], runs(n3, H)] - (y[np.arange(H)[:, None], runs(n4, H)])))

@@ -1,0 +1,237 @@
+from contextlib import ExitStack
+
+import concourse.mybir as mybir
+
+F32 = mybir.dt.float32
+BF16 = mybir.dt.bfloat16
+I32 = mybir.dt.int32
+U32 = mybir.dt.uint32
+U16 = mybir.dt.uint16
+U8 = mybir.dt.uint8
+FP8X4 = mybir.dt.float8_e4m3fn_x4
+ALU = mybir.AluOpType
+ACT = mybir.ActivationFunctionType
+
+P = 128
+PACK = 4
+T = 2048
+S = 512
+HALF = S // 2
+WINDOW = 2 * S
+FLOPS = 2 * 2 * 512 * 512 * 512
+
+
+def tile_picked_skipjointbminmx_none_p_kernel(
+    tc, x_words, x_scales, w1, gn, w2, offs, n1, n2, n3, n4, out
+):
+    nc = tc.nc
+    with ExitStack() as ctx:
+        lists = ctx.enter_context(tc.tile_pool(name="lists", bufs=1))
+        sb = ctx.enter_context(tc.tile_pool(name="sb", bufs=1))
+        psum = ctx.enter_context(tc.psum_pool(name="psum", bufs=1))
+
+        def tile(shape, dtype, name, tag=None):
+            return sb.tile(shape, dtype, name=name, tag=tag or name, align_bytes=64)
+
+        def halves(list_tile):
+            return [list_tile[:, 0:16], list_tile[:, 16:32]]
+
+        x_scale_table = tile([P, T], U8, "x_scale_table")
+        nc.vector.memset(x_scale_table[:].bitcast(I32), 0)
+
+        w1_rows = w1.rearrange("(p j) c -> p j c", j=PACK)
+        w1_raw = [tile([P, PACK, HALF], F32, "w1_raw%d" % u) for u in range(2)]
+        nc.sync.dma_start(out=w1_raw[0][:], in_=w1_rows[:, :, 0:HALF])
+        for q in range(4):
+            nc.sync.dma_start(
+                out=x_scale_table[32 * q : 32 * q + 4, :].bitcast(I32),
+                in_=x_scales[0, 4 * q : 4 * q + 4, :].bitcast(I32),
+            )
+        offs_list = lists.tile([P, S // 16], U16, name="offs_list")
+        nc.sync.dma_start(offs_list[:], offs)
+        nc.sync.dma_start(out=w1_raw[1][:], in_=w1_rows[:, :, HALF:S])
+        x_word_table = tile([P, T], I32, "x_word_table")
+        nc.sync.dma_start(out=x_word_table[:], in_=x_words[0].rearrange("p c r -> p (c r)").bitcast(I32))
+        gain = tile([P, PACK], F32, "gain")
+        nc.sync.dma_start(out=gain[:], in_=gn.rearrange("(p t) o -> p (t o)", t=PACK))
+        n1_list = lists.tile([P, S // 16], U16, name="n1_list")
+        nc.sync.dma_start(n1_list[:], n1)
+        n2_list = lists.tile([P, S // 16], U16, name="n2_list")
+        nc.sync.dma_start(n2_list[:], n2)
+        w2_raw = tile([P, PACK, S], F32, "w2_raw")
+        nc.sync.dma_start(out=w2_raw[:], in_=w2.rearrange("(p j) c -> p j c", j=PACK))
+        n4_list = lists.tile([P, S // 16], U16, name="n4_list")
+        nc.sync.dma_start(n4_list[:], n4)
+        n3_list = lists.tile([P, S // 16], U16, name="n3_list")
+        nc.sync.dma_start(n3_list[:], n3)
+
+        scaled = [tile([P, WINDOW], F32, "scaled%d" % t) for t in range(PACK)]
+        plain = [tile([P, WINDOW], F32, "plain%d" % t) for t in range(PACK)]
+        for window in scaled + plain:
+            nc.vector.memset(window[:, S:WINDOW], 0.0)
+
+        w1_grouped = tile([P, PACK * P * PACK], BF16, "w1_grouped")
+        w1_dealt = w1_grouped[:].rearrange("p (t m j) -> p m j t", t=PACK, j=PACK)
+        nc.scalar.copy(out=w1_dealt[:, 0:64], in_=w1_raw[0][:].rearrange("p j (m t) -> p m j t", t=PACK))
+        x_scale_picked = tile([P, S], U8, "x_scale_picked")
+        nc.vector.tensor_copy(x_scale_picked[:], x_scale_table[:].indirect(offs_list[:]))
+        nc.vector.tensor_copy(out=w1_dealt[:, 64:128], in_=w1_raw[1][:].rearrange("p j (m t) -> p m j t", t=PACK))
+
+        sign = tile([P, PACK], F32, "sign")
+        nonneg = tile([P, PACK], F32, "nonneg")
+        size = tile([P, PACK], F32, "size")
+        nc.vector.tensor_scalar(nonneg[:], gain[:], 0.0, 2.0, ALU.is_ge, ALU.mult)
+        nc.vector.tensor_scalar(sign[:], nonneg[:], -1.0, None, ALU.add)
+        nc.vector.tensor_tensor(size[:], gain[:], sign[:], ALU.mult)
+
+        w1_codes = tile([P, S], U32, "w1_codes")
+        w1_scales = tile([P, S], U8, "w1_scales")
+        nc.vector.quantize_mx(out=w1_codes[:].bitcast(FP8X4), scales=w1_scales[:], in_=w1_grouped[:])
+
+        x_word_picked = tile([P, S], U32, "x_word_picked")
+        for u in range(2):
+            nc.vector.tensor_copy(
+                x_word_picked[:, u * HALF : (u + 1) * HALF],
+                x_word_table[:].bitcast(U32).indirect(halves(offs_list)[u]),
+            )
+
+        def product(bank, codes, scales, t, moving, moving_scales, cols):
+            rows = slice(t * P, (t + 1) * P)
+            nc.tensor.matmul_mx(
+                out=bank,
+                lhsT=codes[:, rows].bitcast(FP8X4),
+                lhsT_scale=scales[:, rows],
+                rhs=moving[:, cols].bitcast(FP8X4),
+                rhs_scale=moving_scales[:, cols],
+                start=True,
+                stop=True,
+            )
+
+        y_parts = []
+        for t in range(PACK):
+            cuts = [slice(0, HALF), slice(HALF, S)] if t == 0 else [slice(0, S)]
+            parts = []
+            for u, cols in enumerate(cuts):
+                bank = psum.tile([P, cols.stop - cols.start], F32, name="y%d_%d" % (t, u), tag="y%d_%d" % (t, u))
+                product(bank[:], w1_codes, w1_scales, t, x_word_picked, x_scale_picked, cols)
+                parts.append((bank, cols))
+            y_parts.append(parts)
+
+        own = [tile([P, S], BF16, "own%d" % t) for t in range(PACK)]
+
+        def scale_out(t, target):
+            for bank, cols in y_parts[t]:
+                nc.scalar.activation(out=target[:, cols], in_=bank[:], func=ACT.Copy, scale=size[:, t : t + 1])
+
+        def copy_out(t):
+            for bank, cols in y_parts[t]:
+                nc.scalar.copy(out=plain[t][:, cols], in_=bank[:])
+
+        scale_out(0, scaled[0])
+        for t in range(1, PACK):
+            scale_out(t, scaled[t])
+            if t == PACK - 1:
+                scale_out(t - 1, own[t - 1])
+                copy_out(0)
+                copy_out(1)
+                scale_out(t, own[t])
+            else:
+                scale_out(t - 1, own[t - 1])
+        copy_out(2)
+        copy_out(3)
+
+        w2_grouped = [tile([P, 2 * P * PACK], BF16, "w2_grouped0", "w1_codes"), tile([P, 2 * P * PACK], BF16, "w2_grouped1", "w1_scales")]
+        w2_dealt = w2_raw[:].rearrange("p j (m t) -> p m j t", t=PACK)
+        for u in range(2):
+            nc.scalar.copy(
+                out=w2_grouped[u][:].rearrange("p (t m j) -> p m j t", t=2, j=PACK),
+                in_=w2_dealt[:, :, :, 2 * u : 2 * u + 2],
+            )
+
+        first = [tile([P, S], BF16, "first%d" % t) for t in range(PACK)]
+        second = [tile([P, S], BF16, "second%d" % t) for t in range(PACK)]
+        larger = [tile([P, S], BF16, "larger%d" % t) for t in range(PACK)]
+        chosen = []
+
+        def choose(t, tag):
+            chosen.append(tile([P, S], BF16, "chosen%d" % t, tag))
+            nc.vector.tensor_tensor(chosen[t][:], larger[t][:], second[t][:], ALU.min)
+
+        for t in range(PACK):
+            nc.vector.tensor_copy(first[t][:], scaled[t][:].indirect(n1_list[:]))
+            nc.vector.tensor_copy(second[t][:], scaled[t][:].indirect(n2_list[:]))
+            if t > 0:
+                choose(t - 1, "scaled%d" % t)
+            nc.vector.tensor_tensor(larger[t][:], first[t][:], own[t][:], ALU.max)
+
+        fourth = {}
+
+        def fetch_fourth(t, tag):
+            fourth[t] = tile([P, S], F32, "fourth%d" % t, tag)
+            nc.vector.tensor_copy(fourth[t][:], plain[t][:].indirect(n4_list[:]))
+
+        gate = {}
+
+        def make_gate(t, key, cols, offsets, tag):
+            width = cols.stop - cols.start
+            diff = tile([P, width], F32, "diff" + key, tag)
+            nc.vector.tensor_tensor(diff[:], plain[t][:].indirect(offsets), fourth[t][:, cols], ALU.subtract)
+            gate[key] = (diff, tile([P, width], F32, "gate" + key))
+
+        def squash(key):
+            diff, target = gate[key]
+            nc.scalar.activation(out=target[:], in_=diff[:], func=ACT.Tanh)
+
+        fetch_fourth(0, "first3")
+        choose(3, None)
+        fetch_fourth(1, "second3")
+        whole = slice(0, S)
+        make_gate(0, "0", whole, n3_list[:], None)
+
+        w2_codes = tile([P, S], U32, "w2_codes")
+        w2_scales = tile([P, S], U8, "w2_scales")
+        for u in range(2):
+            cols = slice(u * HALF, (u + 1) * HALF)
+            nc.vector.quantize_mx(out=w2_codes[:, cols].bitcast(FP8X4), scales=w2_scales[:, cols], in_=w2_grouped[u][:])
+        make_gate(1, "1", whole, n3_list[:], None)
+
+        z_rows = tile([P, PACK, S], BF16, "z_rows")
+        for t in range(PACK):
+            nc.scalar.activation(out=z_rows[:, t, :], in_=chosen[t][:], func=ACT.Copy, scale=sign[:, t : t + 1])
+        z_grouped = tile([P, S * PACK], BF16, "z_grouped")
+        nc.scalar.copy(
+            out=z_grouped[:].rearrange("p (c i t) -> p c t i", i=4, t=PACK),
+            in_=z_rows[:].rearrange("p t (c i) -> p c t i", i=4),
+        )
+        z_codes = tile([P, S], U32, "z_codes")
+        z_scales = tile([P, S], U8, "z_scales")
+        nc.vector.quantize_mx(out=z_codes[:].bitcast(FP8X4), scales=z_scales[:], in_=z_grouped[:])
+        h = []
+        for t in range(PACK):
+            bank = psum.tile([P, S], F32, name="h%d" % t, tag="h%d" % t if t < PACK - 1 else "y0_0")
+            product(bank[:], w2_codes, w2_scales, t, z_codes, z_scales, whole)
+            h.append(bank)
+
+        out_rows = out.rearrange("(p t) s -> p t s", t=PACK)
+
+        def finish(t, key, cols):
+            result = tile([P, cols.stop - cols.start], F32, "result" + key)
+            nc.vector.tensor_tensor(result[:], h[t][:, cols], gate[key][1][:], ALU.mult)
+            nc.sync.dma_start(out=out_rows[:, t, cols], in_=result[:])
+
+        squash("0")
+        squash("1")
+        fetch_fourth(2, "z_grouped")
+        fetch_fourth(3, "z_rows")
+        make_gate(2, "2", whole, n3_list[:], None)
+        squash("2")
+        finish(0, "0", whole)
+        finish(1, "1", whole)
+        left, right = slice(0, HALF), slice(HALF, S)
+        make_gate(3, "3a", left, halves(n3_list)[0], "gate1")
+        squash("3a")
+        finish(2, "2", whole)
+        make_gate(3, "3b", right, halves(n3_list)[1], "gate2")
+        squash("3b")
+        finish(3, "3a", left)
+        finish(3, "3b", right)

@@ -38,28 +38,25 @@ def tile_picked_skipjointbminmx_none_p_kernel(
 
         x_scale_table = tile([P, T], U8, "x_scale_table")
         nc.vector.memset(x_scale_table[:].bitcast(I32), 0)
+        x_scale_stage = tile([P, T], U8, "x_scale_stage")
 
-        w1_rows = w1.rearrange("(p j) c -> p j c", j=PACK)
-        w1_raw = [tile([P, PACK, HALF], F32, "w1_raw%d" % u) for u in range(2)]
-        nc.sync.dma_start(out=w1_raw[0][:], in_=w1_rows[:, :, 0:HALF])
         for q in range(4):
             nc.sync.dma_start(
-                out=x_scale_table[32 * q : 32 * q + 4, :].bitcast(I32),
+                out=x_scale_stage[32 * q : 32 * q + 4, :].bitcast(I32),
                 in_=x_scales[0, 4 * q : 4 * q + 4, :].bitcast(I32),
             )
         offs_list = lists.tile([P, S // 16], U16, name="offs_list")
         nc.sync.dma_start(offs_list[:], offs)
-        nc.sync.dma_start(out=w1_raw[1][:], in_=w1_rows[:, :, HALF:S])
+        w1_raw = tile([P, PACK, S], F32, "w1_raw")
+        nc.sync.dma_start(out=w1_raw[:], in_=w1.rearrange("(p j) c -> p j c", j=PACK))
         x_word_table = tile([P, T], I32, "x_word_table")
         nc.sync.dma_start(out=x_word_table[:], in_=x_words[0].rearrange("p c r -> p (c r)").bitcast(I32))
         gain = tile([P, PACK], F32, "gain")
-        nc.sync.dma_start(out=gain[:], in_=gn.rearrange("(p t) o -> p (t o)", t=PACK))
+        nc.scalar.dma_start(out=gain[:], in_=gn.rearrange("(p t) o -> p (t o)", t=PACK))
         n1_list = lists.tile([P, S // 16], U16, name="n1_list")
         nc.sync.dma_start(n1_list[:], n1)
         n2_list = lists.tile([P, S // 16], U16, name="n2_list")
         nc.sync.dma_start(n2_list[:], n2)
-        w2_raw = tile([P, PACK, S], F32, "w2_raw")
-        nc.sync.dma_start(out=w2_raw[:], in_=w2.rearrange("(p j) c -> p j c", j=PACK))
         n4_list = lists.tile([P, S // 16], U16, name="n4_list")
         nc.sync.dma_start(n4_list[:], n4)
         n3_list = lists.tile([P, S // 16], U16, name="n3_list")
@@ -67,15 +64,23 @@ def tile_picked_skipjointbminmx_none_p_kernel(
 
         scaled = [tile([P, WINDOW], F32, "scaled%d" % t) for t in range(PACK)]
         plain = [tile([P, WINDOW], F32, "plain%d" % t) for t in range(PACK)]
-        for window in scaled + plain:
-            nc.vector.memset(window[:, S:WINDOW], 0.0)
+        for window in scaled:
+            nc.gpsimd.memset(window[:, S:WINDOW], 0.0)
+        for window in plain:
+            nc.scalar.copy(out=window[:, S:WINDOW], in_=scaled[0][:, S:WINDOW])
 
-        w1_grouped = tile([P, PACK * P * PACK], BF16, "w1_grouped")
-        w1_dealt = w1_grouped[:].rearrange("p (t m j) -> p m j t", t=PACK, j=PACK)
-        nc.scalar.copy(out=w1_dealt[:, 0:64], in_=w1_raw[0][:].rearrange("p j (m t) -> p m j t", t=PACK))
+        for q in range(4):
+            rows = slice(32 * q, 32 * q + 4)
+            nc.vector.tensor_copy(x_scale_table[rows, :].bitcast(I32), x_scale_stage[rows, :].bitcast(I32))
         x_scale_picked = tile([P, S], U8, "x_scale_picked")
         nc.vector.tensor_copy(x_scale_picked[:], x_scale_table[:].indirect(offs_list[:]))
-        nc.vector.tensor_copy(out=w1_dealt[:, 64:128], in_=w1_raw[1][:].rearrange("p j (m t) -> p m j t", t=PACK))
+        w1_grouped = tile([P, PACK * P * PACK], BF16, "w1_grouped")
+        w1_dealt = w1_grouped[:].rearrange("p (t m j) -> p m j t", t=PACK, j=PACK)
+        w1_source = w1_raw[:].rearrange("p j (m t) -> p m j t", t=PACK)
+        nc.scalar.copy(out=w1_dealt[:, 0:48], in_=w1_source[:, 0:48])
+        nc.vector.tensor_copy(out=w1_dealt[:, 48:128], in_=w1_source[:, 48:128])
+        w2_raw = tile([P, PACK, S], F32, "w2_raw", "w1_raw")
+        nc.sync.dma_start(out=w2_raw[:], in_=w2.rearrange("(p j) c -> p j c", j=PACK))
 
         sign = tile([P, PACK], F32, "sign")
         nonneg = tile([P, PACK], F32, "nonneg")
@@ -117,7 +122,7 @@ def tile_picked_skipjointbminmx_none_p_kernel(
                 parts.append((bank, cols))
             y_parts.append(parts)
 
-        own = [tile([P, S], BF16, "own%d" % t) for t in range(PACK)]
+        own = [tile([P, 2, S], BF16, "own%d" % u) for u in range(2)]
 
         def scale_out(t, target):
             for bank, cols in y_parts[t]:
@@ -127,17 +132,16 @@ def tile_picked_skipjointbminmx_none_p_kernel(
             for bank, cols in y_parts[t]:
                 nc.scalar.copy(out=plain[t][:, cols], in_=bank[:])
 
-        scale_out(0, scaled[0])
-        for t in range(1, PACK):
+        for t in (0, 1):
             scale_out(t, scaled[t])
-            if t == PACK - 1:
-                scale_out(t - 1, own[t - 1])
-                copy_out(0)
-                copy_out(1)
-                scale_out(t, own[t])
-            else:
-                scale_out(t - 1, own[t - 1])
-        copy_out(2)
+        for t in (0, 1):
+            scale_out(t, own[0][:, t])
+        for t in (2, 3):
+            scale_out(t, scaled[t])
+        for t in (0, 1, 2):
+            copy_out(t)
+        for t in (2, 3):
+            scale_out(t, own[1][:, t - 2])
         copy_out(3)
 
         w2_grouped = [tile([P, 2 * P * PACK], BF16, "w2_grouped0", "w1_codes"), tile([P, 2 * P * PACK], BF16, "w2_grouped1", "w1_scales")]
@@ -148,21 +152,26 @@ def tile_picked_skipjointbminmx_none_p_kernel(
                 in_=w2_dealt[:, :, :, 2 * u : 2 * u + 2],
             )
 
-        first = [tile([P, S], BF16, "first%d" % t) for t in range(PACK)]
-        second = [tile([P, S], BF16, "second%d" % t) for t in range(PACK)]
-        larger = [tile([P, S], BF16, "larger%d" % t) for t in range(PACK)]
+        first = [tile([P, 2, S], BF16, "first%d" % u) for u in range(2)]
+        second = [tile([P, 2, S], BF16, "second%d" % u) for u in range(2)]
+        larger = [tile([P, 2, S], BF16, "larger%d" % u) for u in range(2)]
         chosen = []
 
-        def choose(t, tag):
-            chosen.append(tile([P, S], BF16, "chosen%d" % t, tag))
-            nc.vector.tensor_tensor(chosen[t][:], larger[t][:], second[t][:], ALU.min)
+        def fetch_pair(t):
+            nc.vector.tensor_copy(first[t // 2][:, t % 2], scaled[t][:].indirect(n1_list[:]))
+            nc.vector.tensor_copy(second[t // 2][:, t % 2], scaled[t][:].indirect(n2_list[:]))
 
-        for t in range(PACK):
-            nc.vector.tensor_copy(first[t][:], scaled[t][:].indirect(n1_list[:]))
-            nc.vector.tensor_copy(second[t][:], scaled[t][:].indirect(n2_list[:]))
-            if t > 0:
-                choose(t - 1, "scaled%d" % t)
-            nc.vector.tensor_tensor(larger[t][:], first[t][:], own[t][:], ALU.max)
+        def choose(u, tag):
+            chosen.append(tile([P, 2, S], BF16, "chosen%d" % u, tag))
+            nc.vector.tensor_tensor(chosen[u][:], larger[u][:], second[u][:], ALU.min)
+
+        fetch_pair(0)
+        fetch_pair(1)
+        nc.vector.tensor_tensor(larger[0][:], first[0][:], own[0][:], ALU.max)
+        fetch_pair(2)
+        choose(0, "scaled2")
+        fetch_pair(3)
+        nc.vector.tensor_tensor(larger[1][:], first[1][:], own[1][:], ALU.max)
 
         fourth = {}
 
@@ -182,9 +191,9 @@ def tile_picked_skipjointbminmx_none_p_kernel(
             diff, target = gate[key]
             nc.scalar.activation(out=target[:], in_=diff[:], func=ACT.Tanh)
 
-        fetch_fourth(0, "first3")
-        choose(3, None)
-        fetch_fourth(1, "second3")
+        fetch_fourth(0, "first1")
+        choose(1, None)
+        fetch_fourth(1, "second1")
         whole = slice(0, S)
         make_gate(0, "0", whole, n3_list[:], None)
 
@@ -194,10 +203,11 @@ def tile_picked_skipjointbminmx_none_p_kernel(
             cols = slice(u * HALF, (u + 1) * HALF)
             nc.vector.quantize_mx(out=w2_codes[:, cols].bitcast(FP8X4), scales=w2_scales[:, cols], in_=w2_grouped[u][:])
         make_gate(1, "1", whole, n3_list[:], None)
+        fetch_fourth(2, "larger1")
 
         z_rows = tile([P, PACK, S], BF16, "z_rows")
         for t in range(PACK):
-            nc.scalar.activation(out=z_rows[:, t, :], in_=chosen[t][:], func=ACT.Copy, scale=sign[:, t : t + 1])
+            nc.scalar.activation(out=z_rows[:, t, :], in_=chosen[t // 2][:, t % 2], func=ACT.Copy, scale=sign[:, t : t + 1])
         z_grouped = tile([P, S * PACK], BF16, "z_grouped")
         nc.scalar.copy(
             out=z_grouped[:].rearrange("p (c i t) -> p c t i", i=4, t=PACK),
@@ -221,9 +231,8 @@ def tile_picked_skipjointbminmx_none_p_kernel(
 
         squash("0")
         squash("1")
-        fetch_fourth(2, "z_grouped")
+        make_gate(2, "2", whole, n3_list[:], "z_grouped")
         fetch_fourth(3, "z_rows")
-        make_gate(2, "2", whole, n3_list[:], None)
         squash("2")
         finish(0, "0", whole)
         finish(1, "1", whole)

@@ -62,6 +62,9 @@ def tile_picked_skipjointbminmx_none_p_kernel(
         n3_list = lists.tile([P, S // 16], U16, name="n3_list")
         nc.sync.dma_start(n3_list[:], n3)
 
+        warm = tile([P, 1], F32, "warm")
+        nc.gpsimd.memset(warm[:], 0.0)
+        nc.scalar.activation(out=warm[:], in_=warm[:], func=ACT.Tanh)
         scaled = [tile([P, WINDOW], F32, "scaled%d" % t) for t in range(PACK)]
         plain = [tile([P, WINDOW], F32, "plain%d" % t) for t in range(PACK)]
         for window in scaled:
@@ -77,27 +80,35 @@ def tile_picked_skipjointbminmx_none_p_kernel(
         w1_grouped = tile([P, PACK * P * PACK], BF16, "w1_grouped")
         w1_dealt = w1_grouped[:].rearrange("p (t m j) -> p m j t", t=PACK, j=PACK)
         w1_source = w1_raw[:].rearrange("p j (m t) -> p m j t", t=PACK)
-        nc.scalar.copy(out=w1_dealt[:, 0:48], in_=w1_source[:, 0:48])
-        nc.vector.tensor_copy(out=w1_dealt[:, 48:128], in_=w1_source[:, 48:128])
+        nc.scalar.copy(out=w1_dealt[:, 0:64], in_=w1_source[:, 0:64])
+        nc.vector.tensor_copy(out=w1_dealt[:, 64:128], in_=w1_source[:, 64:128])
         w2_raw = tile([P, PACK, S], F32, "w2_raw", "w1_raw")
         nc.sync.dma_start(out=w2_raw[:], in_=w2.rearrange("(p j) c -> p j c", j=PACK))
 
         sign = tile([P, PACK], F32, "sign")
-        nonneg = tile([P, PACK], F32, "nonneg")
         size = tile([P, PACK], F32, "size")
-        nc.vector.tensor_scalar(nonneg[:], gain[:], 0.0, 2.0, ALU.is_ge, ALU.mult)
-        nc.vector.tensor_scalar(sign[:], nonneg[:], -1.0, None, ALU.add)
-        nc.vector.tensor_tensor(size[:], gain[:], sign[:], ALU.mult)
+        nc.scalar.activation(out=size[:], in_=gain[:], func=ACT.Abs)
+        nc.scalar.activation(out=sign[:], in_=gain[:], func=ACT.Sign)
 
-        w1_codes = tile([P, S], U32, "w1_codes")
-        w1_scales = tile([P, S], U8, "w1_scales")
-        nc.vector.quantize_mx(out=w1_codes[:].bitcast(FP8X4), scales=w1_scales[:], in_=w1_grouped[:])
+        w1_head_codes = tile([P, P], U32, "w1_head_codes")
+        w1_head_scales = tile([P, P], U8, "w1_head_scales")
+        nc.vector.quantize_mx(out=w1_head_codes[:].bitcast(FP8X4), scales=w1_head_scales[:], in_=w1_grouped[:, 0 : P * PACK])
 
         x_word_picked = tile([P, S], U32, "x_word_picked")
         for u in range(2):
             nc.vector.tensor_copy(
                 x_word_picked[:, u * HALF : (u + 1) * HALF],
                 x_word_table[:].bitcast(U32).indirect(halves(offs_list)[u]),
+            )
+
+        w1_codes = tile([P, S], U32, "w1_codes", "x_word_table")
+        w1_scales = tile([P, S], U8, "w1_scales")
+        for first_tile, end_tile in ((1, 2), (2, 4)):
+            cols = slice(first_tile * P, end_tile * P)
+            nc.vector.quantize_mx(
+                out=w1_codes[:, cols].bitcast(FP8X4),
+                scales=w1_scales[:, cols],
+                in_=w1_grouped[:, cols.start * PACK : cols.stop * PACK],
             )
 
         def product(bank, codes, scales, t, moving, moving_scales, cols):
@@ -118,7 +129,8 @@ def tile_picked_skipjointbminmx_none_p_kernel(
             parts = []
             for u, cols in enumerate(cuts):
                 bank = psum.tile([P, cols.stop - cols.start], F32, name="y%d_%d" % (t, u), tag="y%d_%d" % (t, u))
-                product(bank[:], w1_codes, w1_scales, t, x_word_picked, x_scale_picked, cols)
+                codes, scales = (w1_head_codes, w1_head_scales) if t == 0 else (w1_codes, w1_scales)
+                product(bank[:], codes, scales, t, x_word_picked, x_scale_picked, cols)
                 parts.append((bank, cols))
             y_parts.append(parts)
 
@@ -144,7 +156,7 @@ def tile_picked_skipjointbminmx_none_p_kernel(
             scale_out(t, own[1][:, t - 2])
         copy_out(3)
 
-        w2_grouped = [tile([P, 2 * P * PACK], BF16, "w2_grouped0", "w1_codes"), tile([P, 2 * P * PACK], BF16, "w2_grouped1", "w1_scales")]
+        w2_grouped = [tile([P, 2 * P * PACK], BF16, "w2_grouped0", "x_word_table"), tile([P, 2 * P * PACK], BF16, "w2_grouped1", "w1_scales")]
         w2_dealt = w2_raw[:].rearrange("p j (m t) -> p m j t", t=PACK)
         for u in range(2):
             nc.scalar.copy(
@@ -239,8 +251,8 @@ def tile_picked_skipjointbminmx_none_p_kernel(
         left, right = slice(0, HALF), slice(HALF, S)
         make_gate(3, "3a", left, halves(n3_list)[0], "gate1")
         squash("3a")
-        finish(2, "2", whole)
-        make_gate(3, "3b", right, halves(n3_list)[1], "gate2")
+        make_gate(3, "3b", right, halves(n3_list)[1], "gate0")
         squash("3b")
+        finish(2, "2", whole)
         finish(3, "3a", left)
         finish(3, "3b", right)

@@ -41,7 +41,7 @@ def tile_picked_skipjointbminmx_none_p_kernel(
         x_scale_stage = tile([P, T], U8, "x_scale_stage")
 
         for q in range(4):
-            nc.sync.dma_start(
+            (nc.sync if q < 2 else nc.scalar).dma_start(
                 out=x_scale_stage[32 * q : 32 * q + 4, :].bitcast(I32),
                 in_=x_scales[0, 4 * q : 4 * q + 4, :].bitcast(I32),
             )
@@ -63,12 +63,11 @@ def tile_picked_skipjointbminmx_none_p_kernel(
         nc.sync.dma_start(n3_list[:], n3)
 
         warm = tile([P, 1], F32, "warm")
-        nc.gpsimd.memset(warm[:], 0.0)
-        nc.scalar.activation(out=warm[:], in_=warm[:], func=ACT.Tanh)
         scaled = [tile([P, WINDOW], F32, "scaled%d" % t) for t in range(PACK)]
         plain = [tile([P, WINDOW], F32, "plain%d" % t) for t in range(PACK)]
         for window in scaled:
-            nc.gpsimd.memset(window[:, S:WINDOW], 0.0)
+            nc.vector.memset(window[:, S:WINDOW], 0.0)
+        nc.scalar.activation(out=warm[:], in_=scaled[0][:, S : S + 1], func=ACT.Tanh)
         for window in plain:
             nc.scalar.copy(out=window[:, S:WINDOW], in_=scaled[0][:, S:WINDOW])
 
@@ -245,14 +244,18 @@ def tile_picked_skipjointbminmx_none_p_kernel(
         squash("1")
         make_gate(2, "2", whole, n3_list[:], "z_grouped")
         fetch_fourth(3, "z_rows")
-        squash("2")
+        left, right = slice(0, HALF), slice(HALF, S)
+        diff2 = gate["2"][0]
+        for key, cols in (("2a", left), ("2b", right)):
+            gate[key] = (diff2[:, cols], tile([P, HALF], F32, "gate" + key))
+            nc.scalar.activation(out=gate[key][1][:], in_=diff2[:, cols], func=ACT.Tanh)
         finish(0, "0", whole)
         finish(1, "1", whole)
-        left, right = slice(0, HALF), slice(HALF, S)
         make_gate(3, "3a", left, halves(n3_list)[0], "gate1")
         squash("3a")
-        make_gate(3, "3b", right, halves(n3_list)[1], "gate0")
+        finish(2, "2a", left)
+        make_gate(3, "3b", right, halves(n3_list)[1], "gate2a")
         squash("3b")
-        finish(2, "2", whole)
+        finish(2, "2b", right)
         finish(3, "3a", left)
         finish(3, "3b", right)

from contextlib import ExitStack

import concourse.mybir as mybir

F32 = mybir.dt.float32
BF16 = mybir.dt.bfloat16
I32 = mybir.dt.int32
U32 = mybir.dt.uint32
U16 = mybir.dt.uint16
U8 = mybir.dt.uint8
FP8X4 = mybir.dt.float8_e4m3fn_x4
ALU = mybir.AluOpType
ACT = mybir.ActivationFunctionType

P = 128
PACK = 4
T = 2048
S = 512
HALF = S // 2
WINDOW = 2 * S
FLOPS = 2 * 2 * 512 * 512 * 512


def tile_picked_skipjointbminmx_none_p_kernel(
    tc, x_words, x_scales, w1, gn, w2, offs, n1, n2, n3, n4, out
):
    nc = tc.nc
    with ExitStack() as ctx:
        lists = ctx.enter_context(tc.tile_pool(name="lists", bufs=1))
        sb = ctx.enter_context(tc.tile_pool(name="sb", bufs=1))
        psum = ctx.enter_context(tc.psum_pool(name="psum", bufs=1))

        def tile(shape, dtype, name, tag=None):
            return sb.tile(shape, dtype, name=name, tag=tag or name, align_bytes=64)

        def halves(list_tile):
            return [list_tile[:, 0:16], list_tile[:, 16:32]]

        x_scale_table = tile([P, T], U8, "x_scale_table")
        nc.vector.memset(x_scale_table[:].bitcast(I32), 0)
        x_scale_stage = tile([P, T], U8, "x_scale_stage")

        for q in range(4):
            (nc.sync if q < 2 else nc.scalar).dma_start(
                out=x_scale_stage[32 * q : 32 * q + 4, :].bitcast(I32),
                in_=x_scales[0, 4 * q : 4 * q + 4, :].bitcast(I32),
            )
        offs_list = lists.tile([P, S // 16], U16, name="offs_list")
        nc.sync.dma_start(offs_list[:], offs)
        w1_raw = tile([P, PACK, S], F32, "w1_raw")
        nc.sync.dma_start(out=w1_raw[:], in_=w1.rearrange("(p j) c -> p j c", j=PACK))
        x_word_table = tile([P, T], I32, "x_word_table")
        nc.sync.dma_start(out=x_word_table[:], in_=x_words[0].rearrange("p c r -> p (c r)").bitcast(I32))
        gain = tile([P, PACK], F32, "gain")
        nc.scalar.dma_start(out=gain[:], in_=gn.rearrange("(p t) o -> p (t o)", t=PACK))
        n1_list = lists.tile([P, S // 16], U16, name="n1_list")
        nc.sync.dma_start(n1_list[:], n1)
        n2_list = lists.tile([P, S // 16], U16, name="n2_list")
        nc.sync.dma_start(n2_list[:], n2)
        n4_list = lists.tile([P, S // 16], U16, name="n4_list")
        nc.sync.dma_start(n4_list[:], n4)
        n3_list = lists.tile([P, S // 16], U16, name="n3_list")
        nc.sync.dma_start(n3_list[:], n3)

        warm = tile([P, 1], F32, "warm")
        scaled = [tile([P, WINDOW], F32, "scaled%d" % t) for t in range(PACK)]
        plain = [tile([P, WINDOW], F32, "plain%d" % t) for t in range(PACK)]
        for window in scaled:
            nc.vector.memset(window[:, S:WINDOW], 0.0)
        nc.scalar.activation(out=warm[:], in_=scaled[0][:, S : S + 1], func=ACT.Tanh)
        for window in plain:
            nc.scalar.copy(out=window[:, S:WINDOW], in_=scaled[0][:, S:WINDOW])

        for q in range(4):
            rows = slice(32 * q, 32 * q + 4)
            nc.vector.tensor_copy(x_scale_table[rows, :].bitcast(I32), x_scale_stage[rows, :].bitcast(I32))
        x_scale_picked = tile([P, S], U8, "x_scale_picked")
        nc.vector.tensor_copy(x_scale_picked[:], x_scale_table[:].indirect(offs_list[:]))
        w1_grouped = tile([P, PACK * P * PACK], BF16, "w1_grouped")
        w1_dealt = w1_grouped[:].rearrange("p (t m j) -> p m j t", t=PACK, j=PACK)
        w1_source = w1_raw[:].rearrange("p j (m t) -> p m j t", t=PACK)
        nc.scalar.copy(out=w1_dealt[:, 0:64], in_=w1_source[:, 0:64])
        nc.vector.tensor_copy(out=w1_dealt[:, 64:128], in_=w1_source[:, 64:128])
        w2_raw = tile([P, PACK, S], F32, "w2_raw", "w1_raw")
        nc.sync.dma_start(out=w2_raw[:], in_=w2.rearrange("(p j) c -> p j c", j=PACK))

        sign = tile([P, PACK], F32, "sign")
        size = tile([P, PACK], F32, "size")
        nc.scalar.activation(out=size[:], in_=gain[:], func=ACT.Abs)
        nc.scalar.activation(out=sign[:], in_=gain[:], func=ACT.Sign)

        w1_head_codes = tile([P, P], U32, "w1_head_codes")
        w1_head_scales = tile([P, P], U8, "w1_head_scales")
        nc.vector.quantize_mx(out=w1_head_codes[:].bitcast(FP8X4), scales=w1_head_scales[:], in_=w1_grouped[:, 0 : P * PACK])

        x_word_picked = tile([P, S], U32, "x_word_picked")
        for u in range(2):
            nc.vector.tensor_copy(
                x_word_picked[:, u * HALF : (u + 1) * HALF],
                x_word_table[:].bitcast(U32).indirect(halves(offs_list)[u]),
            )

        w1_codes = tile([P, S], U32, "w1_codes", "x_word_table")
        w1_scales = tile([P, S], U8, "w1_scales")
        for first_tile, end_tile in ((1, 2), (2, 4)):
            cols = slice(first_tile * P, end_tile * P)
            nc.vector.quantize_mx(
                out=w1_codes[:, cols].bitcast(FP8X4),
                scales=w1_scales[:, cols],
                in_=w1_grouped[:, cols.start * PACK : cols.stop * PACK],
            )

        def product(bank, codes, scales, t, moving, moving_scales, cols):
            rows = slice(t * P, (t + 1) * P)
            nc.tensor.matmul_mx(
                out=bank,
                lhsT=codes[:, rows].bitcast(FP8X4),
                lhsT_scale=scales[:, rows],
                rhs=moving[:, cols].bitcast(FP8X4),
                rhs_scale=moving_scales[:, cols],
                start=True,
                stop=True,
            )

        y_parts = []
        for t in range(PACK):
            cuts = [slice(0, HALF), slice(HALF, S)] if t == 0 else [slice(0, S)]
            parts = []
            for u, cols in enumerate(cuts):
                bank = psum.tile([P, cols.stop - cols.start], F32, name="y%d_%d" % (t, u), tag="y%d_%d" % (t, u))
                codes, scales = (w1_head_codes, w1_head_scales) if t == 0 else (w1_codes, w1_scales)
                product(bank[:], codes, scales, t, x_word_picked, x_scale_picked, cols)
                parts.append((bank, cols))
            y_parts.append(parts)

        own = [tile([P, 2, S], BF16, "own%d" % u) for u in range(2)]

        def scale_out(t, target):
            for bank, cols in y_parts[t]:
                nc.scalar.activation(out=target[:, cols], in_=bank[:], func=ACT.Copy, scale=size[:, t : t + 1])

        def copy_out(t):
            for bank, cols in y_parts[t]:
                nc.scalar.copy(out=plain[t][:, cols], in_=bank[:])

        for t in (0, 1):
            scale_out(t, scaled[t])
        for t in (0, 1):
            scale_out(t, own[0][:, t])
        for t in (2, 3):
            scale_out(t, scaled[t])
        for t in (0, 1, 2):
            copy_out(t)
        for t in (2, 3):
            scale_out(t, own[1][:, t - 2])
        copy_out(3)

        w2_grouped = [tile([P, 2 * P * PACK], BF16, "w2_grouped0", "x_word_table"), tile([P, 2 * P * PACK], BF16, "w2_grouped1", "w1_scales")]
        w2_dealt = w2_raw[:].rearrange("p j (m t) -> p m j t", t=PACK)
        for u in range(2):
            nc.scalar.copy(
                out=w2_grouped[u][:].rearrange("p (t m j) -> p m j t", t=2, j=PACK),
                in_=w2_dealt[:, :, :, 2 * u : 2 * u + 2],
            )

        first = [tile([P, 2, S], BF16, "first%d" % u) for u in range(2)]
        second = [tile([P, 2, S], BF16, "second%d" % u) for u in range(2)]
        larger = [tile([P, 2, S], BF16, "larger%d" % u) for u in range(2)]
        chosen = []

        def fetch_pair(t):
            nc.vector.tensor_copy(first[t // 2][:, t % 2], scaled[t][:].indirect(n1_list[:]))
            nc.vector.tensor_copy(second[t // 2][:, t % 2], scaled[t][:].indirect(n2_list[:]))

        def choose(u, tag):
            chosen.append(tile([P, 2, S], BF16, "chosen%d" % u, tag))
            nc.vector.tensor_tensor(chosen[u][:], larger[u][:], second[u][:], ALU.min)

        fetch_pair(0)
        fetch_pair(1)
        nc.vector.tensor_tensor(larger[0][:], first[0][:], own[0][:], ALU.max)
        fetch_pair(2)
        choose(0, "scaled2")
        fetch_pair(3)
        nc.vector.tensor_tensor(larger[1][:], first[1][:], own[1][:], ALU.max)

        fourth = {}

        def fetch_fourth(t, tag):
            fourth[t] = tile([P, S], F32, "fourth%d" % t, tag)
            nc.vector.tensor_copy(fourth[t][:], plain[t][:].indirect(n4_list[:]))

        gate = {}

        def make_gate(t, key, cols, offsets, tag):
            width = cols.stop - cols.start
            diff = tile([P, width], F32, "diff" + key, tag)
            nc.vector.tensor_tensor(diff[:], plain[t][:].indirect(offsets), fourth[t][:, cols], ALU.subtract)
            gate[key] = (diff, tile([P, width], F32, "gate" + key))

        def squash(key):
            diff, target = gate[key]
            nc.scalar.activation(out=target[:], in_=diff[:], func=ACT.Tanh)

        fetch_fourth(0, "first1")
        choose(1, None)
        fetch_fourth(1, "second1")
        whole = slice(0, S)
        make_gate(0, "0", whole, n3_list[:], None)

        w2_codes = tile([P, S], U32, "w2_codes")
        w2_scales = tile([P, S], U8, "w2_scales")
        for u in range(2):
            cols = slice(u * HALF, (u + 1) * HALF)
            nc.vector.quantize_mx(out=w2_codes[:, cols].bitcast(FP8X4), scales=w2_scales[:, cols], in_=w2_grouped[u][:])
        make_gate(1, "1", whole, n3_list[:], None)
        fetch_fourth(2, "larger1")

        z_rows = tile([P, PACK, S], BF16, "z_rows")
        for t in range(PACK):
            nc.scalar.activation(out=z_rows[:, t, :], in_=chosen[t // 2][:, t % 2], func=ACT.Copy, scale=sign[:, t : t + 1])
        z_grouped = tile([P, S * PACK], BF16, "z_grouped")
        nc.scalar.copy(
            out=z_grouped[:].rearrange("p (c i t) -> p c t i", i=4, t=PACK),
            in_=z_rows[:].rearrange("p t (c i) -> p c t i", i=4),
        )
        z_codes = tile([P, S], U32, "z_codes")
        z_scales = tile([P, S], U8, "z_scales")
        nc.vector.quantize_mx(out=z_codes[:].bitcast(FP8X4), scales=z_scales[:], in_=z_grouped[:])
        h = []
        for t in range(PACK):
            bank = psum.tile([P, S], F32, name="h%d" % t, tag="h%d" % t if t < PACK - 1 else "y0_0")
            product(bank[:], w2_codes, w2_scales, t, z_codes, z_scales, whole)
            h.append(bank)

        out_rows = out.rearrange("(p t) s -> p t s", t=PACK)

        def finish(t, key, cols):
            result = tile([P, cols.stop - cols.start], F32, "result" + key)
            nc.vector.tensor_tensor(result[:], h[t][:, cols], gate[key][1][:], ALU.mult)
            nc.sync.dma_start(out=out_rows[:, t, cols], in_=result[:])

        squash("0")
        squash("1")
        make_gate(2, "2", whole, n3_list[:], "z_grouped")
        fetch_fourth(3, "z_rows")
        left, right = slice(0, HALF), slice(HALF, S)
        diff2 = gate["2"][0]
        for key, cols in (("2a", left), ("2b", right)):
            gate[key] = (diff2[:, cols], tile([P, HALF], F32, "gate" + key))
            nc.scalar.activation(out=gate[key][1][:], in_=diff2[:, cols], func=ACT.Tanh)
        finish(0, "0", whole)
        finish(1, "1", whole)
        make_gate(3, "3a", left, halves(n3_list)[0], "gate1")
        squash("3a")
        finish(2, "2a", left)
        make_gate(3, "3b", right, halves(n3_list)[1], "gate2a")
        squash("3b")
        finish(2, "2b", right)
        finish(3, "3a", left)
        finish(3, "3b", right)
